import numpy as np
import ml_dtypes


def mxq(x, axis, fmt="e4m3"):
    dtype, down = {"e4m3": (ml_dtypes.float8_e4m3fn, 7), "e5m2": (ml_dtypes.float8_e5m2, 14)}[fmt]
    v = np.moveaxis(np.asarray(x, np.float32).astype(ml_dtypes.bfloat16).astype(np.float64), axis, -1)
    blocks = v.reshape(v.shape[:-1] + (-1, 32))
    amax = np.abs(blocks).max(-1, keepdims=True)
    byte = np.maximum(np.where(amax > 0, np.frexp(amax)[1] - 1 + 127, 0) - down, 1)
    scale = np.exp2(byte - 127.0)
    codes = (blocks / scale).astype(np.float32).astype(dtype).astype(np.float64)
    return np.moveaxis((codes * scale).reshape(v.shape), -1, axis)


WIDE = False


def mx_kscale(k):
    if not WIDE:
        return np.ones(k)
    levels = np.array([10, -10, 5, -5, 0])
    if k % 512:
        return np.exp2(np.random.permutation(np.resize(levels, k // 32))).repeat(32)
    a = np.empty((k // 512, 16))
    for p in range(k // 512):
        a[p, :8] = np.random.permutation(np.resize(levels, 8))
        for g in range(8):
            far = levels[np.abs(levels - a[p, g]) >= 10]
            a[p, g + 8] = far[np.random.randint(len(far))]
    return np.exp2(a.ravel()).repeat(32)


def f64(x):
    return np.asarray(x).astype(np.float64)


def striped8(idx):
    return np.asarray(idx).reshape(8, -1, 16).transpose(0, 2, 1).reshape(128, -1).astype(np.uint16)


def unstriped8(offs):
    return offs.reshape(8, 16, -1).transpose(0, 2, 1).reshape(8, -1).astype(np.int64)


def pick8(x, idx, run):
    r = np.arange(len(x))
    return x[r[:, None], idx[r % (8 * run) // run]]


E2M1 = np.array([0.0, 0.5, 1.0, 1.5, 2.0, 3.0, 4.0, 6.0, -0.0, -0.5, -1.0, -1.5, -2.0, -3.0, -4.0, -6.0])


def pack_weight(w, fmt):
    k, n = w.shape
    w = f64(np.asarray(w, np.float32).astype(ml_dtypes.bfloat16)).reshape(k // 32, 32, n)
    amax = np.abs(w).max(1)
    if fmt == "e4m3":
        byte = np.frexp(amax)[1] - 1 + 127 - 7
    else:
        mant, ex = np.frexp(amax / 6.0)
        byte = np.where(mant > 0.5, ex, ex - 1) + 127
    byte = np.clip(np.where(amax > 0, byte, 1), 1, 254)
    scaled = (w * np.exp2(127.0 - byte)[:, None, :]).reshape(k, n).astype(np.float32)
    by_word = np.ascontiguousarray(scaled.reshape(k // 512, 128, 4, n).transpose(0, 1, 3, 2))
    if fmt == "e4m3":
        words = by_word.astype(ml_dtypes.float8_e4m3fn).view(np.uint8)
    else:
        c = by_word.astype(ml_dtypes.float4_e2m1fn).view(np.uint8) & 0xF
        words = (c[..., 0::2] | (c[..., 1::2] << 4)).reshape(k // 512, 128, 2 * n)
    return np.ascontiguousarray(words), np.ascontiguousarray(byte.astype(np.uint8).reshape(k // 512, 16, n))


def unpack_weight(words, scales, fmt):
    g, _, n = scales.shape
    words = np.ascontiguousarray(words).reshape(g, 128, n, -1)
    if fmt == "e4m3":
        vals = words.view(ml_dtypes.float8_e4m3fn).astype(np.float64)
    else:
        nib = np.empty((g, 128, n, 4), np.uint8)
        nib[..., 0::2] = words & 0xF
        nib[..., 1::2] = words >> 4
        vals = E2M1[nib]
    vals = vals * np.repeat(np.exp2(scales.astype(np.float64) - 127.0), 8, axis=1)[..., None]
    return vals.transpose(0, 1, 3, 2).reshape(g * 512, n)


D, T, I, Q = 512, 1024, 512, 128


def setup_inputs():
    n = np.random.standard_normal
    idx = np.stack([np.random.permutation(T)[:I] for _ in range(8)])
    idx2 = np.stack([np.random.permutation(T)[:I] for _ in range(8)])
    idx3 = np.stack([np.random.permutation(T)[:I] for _ in range(8)])
    fd = mx_kscale(D)
    keysp = pack_weight(n((D, T)) / fd[:, None], "e2m1")
    return {
        "query": (n((D, Q)) * 0.9 / np.sqrt(D) * fd[:, None]).astype(np.float32),
        "query2": (n((D, Q)) * 0.9 / np.sqrt(D) * fd[:, None]).astype(np.float32),
        "keys_words": keysp[0],
        "keys_scales": keysp[1],
        "lam": (np.random.uniform(0.5, 1.3, (Q, 1))).astype(np.float32),
        "old": (1.0 * n((Q, T))).astype(np.float32),
        "share2": (np.random.uniform(0.4, 1.2, (Q, 1))).astype(np.float32),
        "offs": striped8(idx),
        "offs2": striped8(idx2),
        "offs3": striped8(idx3),
    }


def reference(query, query2, keys_words, keys_scales, lam, old, share2, offs, offs2, offs3):
    idx = unstriped8(offs)
    idx2 = unstriped8(offs2)
    idx3 = unstriped8(offs3)
    keysu = unpack_weight(keys_words, keys_scales, "e2m1")
    queryq = mxq(f64(query), 0, "e4m3")
    a = queryq.T @ keysu
    query2q = mxq(f64(query2), 0, "e4m3")
    b = query2q.T @ keysu
    w = (np.maximum(pick8(a, idx, 16), pick8(b, idx2, 16)) - np.maximum(pick8(a, idx2, 16), pick8(b, idx, 16))) * f64(lam)
    f1 = np.zeros((Q, T))
    f1[np.arange(Q)[:, None], idx[np.arange(Q) % 128 // 16]] = w
    f2 = np.zeros((Q, T))
    f2[np.arange(Q)[:, None], idx3[np.arange(Q) % 128 // 16]] = w
    y = f64(old) + f1 + f2 * f64(share2)
    return y

@@ -1,0 +1,177 @@
+from contextlib import ExitStack
+
+import concourse.mybir as mybir
+from concourse.masks import make_identity
+
+D, T, I, Q = 512, 1024, 512, 128
+FLOPS = 2 * 2 * D * T * Q
+
+F32 = mybir.dt.float32
+BF16 = mybir.dt.bfloat16
+I32 = mybir.dt.int32
+U32 = mybir.dt.uint32
+U16 = mybir.dt.uint16
+U8 = mybir.dt.uint8
+FP8X4 = mybir.dt.float8_e4m3fn_x4
+FP4X4 = mybir.dt.float4_e2m1fn_x4
+ALU = mybir.AluOpType
+COPY = mybir.ActivationFunctionType.Copy
+
+P = 128
+PACK = 4
+BANK = 512
+HALF = I // 2
+QUARTER = I // 4
+GROUP = 16
+OUT_CHUNK = 256
+
+
+def tile_attend_exchanged_lean_twiceput_heads_kernel(
+    tc, query, query2, keys_words, keys_scales, lam, old, share2, offs, offs2, offs3, out
+):
+    nc = tc.nc
+    with ExitStack() as ctx:
+        sb = ctx.enter_context(tc.tile_pool(name="sb", bufs=1))
+        ps = ctx.enter_context(tc.psum_pool(name="ps", bufs=1))
+
+        key_scale = sb.tile([P, T], U8, name="key_scale", align_bytes=64)
+        nc.vector.memset(key_scale[:].bitcast(I32), 0)
+
+        raw = [sb.tile([P, PACK, Q], F32, name="raw%d" % n) for n in range(2)]
+        key_words = sb.tile([P, 2 * T], U8, name="key_words", align_bytes=64)
+        lam_col = sb.tile([P, 1], F32, name="lam_col")
+        nc.sync.dma_start(out=raw[0][:], in_=query.rearrange("(p j) q -> p j q", j=PACK))
+        nc.sync.dma_start(out=key_words[:].bitcast(I32), in_=keys_words[0].bitcast(I32))
+        nc.sync.dma_start(out=raw[1][:], in_=query2.rearrange("(p j) q -> p j q", j=PACK))
+        nc.sync.dma_start(out=lam_col[:], in_=lam)
+        for quad in range(4):
+            nc.scalar.dma_start(
+                out=key_scale[32 * quad : 32 * quad + 4, :].bitcast(I32),
+                in_=keys_scales[0][4 * quad : 4 * quad + 4, :].bitcast(I32),
+            )
+        list1 = sb.tile([P, I // GROUP], U16, name="list1")
+        nc.sync.dma_start(list1[:], offs)
+        list2 = sb.tile([P, I // GROUP], U16, name="list2")
+        nc.sync.dma_start(list2[:], offs2)
+        old_sb = sb.tile([P, T], F32, name="old_sb")
+        nc.sync.dma_start(out=old_sb[:], in_=old)
+        list3 = sb.tile([P, I // GROUP], U16, name="list3")
+        nc.sync.dma_start(list3[:], offs3)
+        share_col = sb.tile([P, 1], F32, name="share_col")
+        nc.sync.dma_start(out=share_col[:], in_=share2)
+
+        f1 = sb.tile([P, T], F32, name="f1")
+        f2 = sb.tile([P, T], F32, name="f2")
+        nc.vector.memset(f1[:], 0.0)
+        nc.vector.memset(f2[:], 0.0)
+        ident = sb.tile([P, P], F32, name="ident")
+        make_identity(nc, ident[:])
+
+        scores = []
+        for n in range(2):
+            grouped = sb.tile([P, Q, PACK], BF16, name="grouped%d" % n, align_bytes=64)
+            nc.vector.tensor_copy(
+                out=grouped[:].rearrange("p (c i) j -> p c j i", i=4),
+                in_=raw[n][:].rearrange("p j (c i) -> p c j i", i=4),
+            )
+            codes = sb.tile([P, Q], U32, name="codes%d" % n, align_bytes=64)
+            q_scale = sb.tile([P, Q], U8, name="q_scale%d" % n, align_bytes=64)
+            nc.vector.quantize_mx(
+                out=codes[:].bitcast(FP8X4),
+                scales=q_scale[:],
+                in_=grouped[:].rearrange("p q j -> p (q j)"),
+            )
+            banks = []
+            for h in range(T // BANK):
+                bank = ps.tile([P, BANK], F32, name="score_bank%d%d" % (n, h), tag="bank%d" % (2 * n + h))
+                nc.tensor.matmul_mx(
+                    out=bank[:],
+                    lhsT=codes[:].bitcast(FP8X4),
+                    lhsT_scale=q_scale[:],
+                    rhs=key_words[:, 2 * BANK * h : 2 * BANK * (h + 1)].bitcast(FP4X4),
+                    rhs_scale=key_scale[:, BANK * h : BANK * (h + 1)],
+                    start=True,
+                    stop=True,
+                )
+                banks.append(bank)
+            scores.append(banks)
+
+        a = sb.tile([P, T], F32, name="a")
+        b = sb.tile([P, T], F32, name="b")
+        lam_row = sb.tile([P, I], F32, name="lam_row")
+        nc.scalar.copy(out=lam_row[:], in_=lam_col[:].to_broadcast([P, I]))
+        nc.vector.tensor_copy(out=a[:, :BANK], in_=scores[0][0][:])
+        nc.scalar.copy(out=a[:, BANK:], in_=scores[0][1][:])
+        nc.scalar.copy(out=b[:, :BANK], in_=scores[1][0][:])
+        nc.scalar.copy(out=b[:, BANK:], in_=scores[1][1][:])
+
+        def entries(lst, lo, hi):
+            return lst[:, lo // GROUP : hi // GROUP]
+
+        ga = [sb.tile([P, 2, HALF], F32, name="ga%d" % h) for h in range(2)]
+        gb = [sb.tile([P, 2, HALF], F32, name="gb%d" % h) for h in range(2)]
+        top = [sb.tile([P, 2, QUARTER], F32, name="top%d" % k) for k in range(4)]
+        diff = sb.tile([P, I], F32, name="diff")
+
+        nc.vector.tensor_copy(out=ga[0][:, 0, :], in_=a[:].indirect(entries(list1, 0, HALF)))
+        nc.vector.tensor_copy(out=ga[0][:, 1, :], in_=a[:].indirect(entries(list2, 0, HALF)))
+        nc.vector.tensor_copy(out=gb[0][:, 0, :], in_=b[:].indirect(entries(list2, 0, HALF)))
+        nc.scalar.activation(gb[0][:, 1, :], b[:].indirect(entries(list1, 0, HALF)), COPY)
+        nc.scalar.activation(ga[1][:, 0, :], a[:].indirect(entries(list1, HALF, I)), COPY)
+        nc.scalar.activation(ga[1][:, 1, :], a[:].indirect(entries(list2, HALF, I)), COPY)
+        nc.scalar.activation(gb[1][:, 0, :], b[:].indirect(entries(list2, HALF, I)), COPY)
+        nc.scalar.activation(gb[1][:, 1, :], b[:].indirect(entries(list1, HALF, I)), COPY)
+
+        chunks = T // OUT_CHUNK
+        blocks = OUT_CHUNK // P
+        turned = [ps.tile([P, OUT_CHUNK], F32, name="turned%d" % k, tag="bank%d" % k) for k in range(chunks)]
+        for k in range(chunks):
+            for j in range(blocks):
+                c = OUT_CHUNK * k + P * j
+                nc.tensor.matmul(
+                    turned[k][:, P * j : P * (j + 1)], old_sb[:, c : c + P], ident[:],
+                    start=(j == 0), stop=False, is_transpose=True,
+                )
+
+        def put(window, lst, lo, hi):
+            nc.vector.tensor_tensor(
+                window[:].indirect(entries(lst, lo, hi)), diff[:, lo:hi], lam_row[:, lo:hi], ALU.mult
+            )
+
+        for h in range(2):
+            for k in (2 * h, 2 * h + 1):
+                part = slice(k % 2 * QUARTER, (k % 2 + 1) * QUARTER)
+                nc.vector.tensor_tensor(top[k][:], ga[h][:, :, part], gb[h][:, :, part], ALU.max)
+            for k in (2 * h, 2 * h + 1):
+                nc.vector.tensor_tensor(
+                    diff[:, k * QUARTER : (k + 1) * QUARTER], top[k][:, 0, :], top[k][:, 1, :], ALU.subtract
+                )
+            for k in (2 * h, 2 * h + 1):
+                put(f1, list1, k * QUARTER, (k + 1) * QUARTER)
+            if h == 0:
+                put(f2, list3, 0, QUARTER)
+        put(f2, list3, QUARTER, I)
+
+        back = []
+        for k in range(chunks):
+            for j in range(blocks):
+                c = OUT_CHUNK * k + P * j
+                nc.tensor.matmul(
+                    turned[k][:, P * j : P * (j + 1)], f1[:, c : c + P], ident[:],
+                    start=False, stop=(j == blocks - 1), is_transpose=True,
+                )
+        for k in range(chunks):
+            staged = sb.tile([P, OUT_CHUNK], F32, name="staged%d" % k)
+            nc.scalar.copy(out=staged[:], in_=turned[k][:])
+            bk = ps.tile([P, OUT_CHUNK], F32, name="back%d" % k)
+            for j in range(blocks):
+                nc.tensor.transpose(bk[:, P * j : P * (j + 1)], staged[:, P * j : P * (j + 1)], ident[:])
+            back.append(bk)
+
+        for k in range(chunks):
+            c = OUT_CHUNK * k
+            res = sb.tile([P, OUT_CHUNK], F32, name="res%d" % k)
+            nc.vector.scalar_tensor_tensor(
+                res[:], f2[:, c : c + OUT_CHUNK], share_col[:], back[k][:], ALU.mult, ALU.add
+            )
+            nc.sync.dma_start(out=out[:, c : c + OUT_CHUNK], in_=res[:])

@@ -23,7 +23,8 @@ BANK = 512
 HALF = I // 2
 QUARTER = I // 4
 GROUP = 16
-OUT_CHUNK = 256
+SPANS = (((0, 512), (512, 768), (768, 1024)), ((0, 256), (256, 512), (512, 768), (768, 1024)))
+OUT_SPANS = ((0, 256), (256, 512), (512, 768), (768, 1024))
 
 
 def tile_attend_exchanged_lean_twiceput_heads_kernel(
@@ -82,14 +83,14 @@ def tile_attend_exchanged_lean_twiceput_heads_kernel(
                 in_=grouped[:].rearrange("p q j -> p (q j)"),
             )
             banks = []
-            for h in range(T // BANK):
-                bank = ps.tile([P, BANK], F32, name="score_bank%d%d" % (n, h), tag="bank%d" % (2 * n + h))
+            for lo, hi in SPANS[n]:
+                bank = ps.tile([P, hi - lo], F32, name="score_bank%d_%d" % (n, lo), tag="bank%d" % (3 * n + len(banks)))
                 nc.tensor.matmul_mx(
                     out=bank[:],
                     lhsT=codes[:].bitcast(FP8X4),
                     lhsT_scale=q_scale[:],
-                    rhs=key_words[:, 2 * BANK * h : 2 * BANK * (h + 1)].bitcast(FP4X4),
-                    rhs_scale=key_scale[:, BANK * h : BANK * (h + 1)],
+                    rhs=key_words[:, 2 * lo : 2 * hi].bitcast(FP4X4),
+                    rhs_scale=key_scale[:, lo:hi],
                     start=True,
                     stop=True,
                 )
@@ -101,14 +102,15 @@ def tile_attend_exchanged_lean_twiceput_heads_kernel(
         lam_row = sb.tile([P, I], F32, name="lam_row")
         nc.scalar.copy(out=lam_row[:], in_=lam_col[:].to_broadcast([P, I]))
         nc.vector.tensor_copy(out=a[:, :BANK], in_=scores[0][0][:])
-        nc.scalar.copy(out=a[:, BANK:], in_=scores[0][1][:])
-        nc.scalar.copy(out=b[:, :BANK], in_=scores[1][0][:])
-        nc.scalar.copy(out=b[:, BANK:], in_=scores[1][1][:])
+        nc.scalar.copy(out=a[:, 512:768], in_=scores[0][1][:])
+        nc.vector.tensor_copy(out=a[:, 768:], in_=scores[0][2][:])
+        for (lo, hi), bank in zip(SPANS[1], scores[1]):
+            nc.scalar.copy(out=b[:, lo:hi], in_=bank[:])
 
         def entries(lst, lo, hi):
             return lst[:, lo // GROUP : hi // GROUP]
 
-        ga = [sb.tile([P, 2, HALF], F32, name="ga%d" % h) for h in range(2)]
+        ga = [sb.tile([P, 2, HALF], F32, name="ga0", tag="ga")]
         gb = [sb.tile([P, 2, HALF], F32, name="gb%d" % h) for h in range(2)]
         top = [sb.tile([P, 2, QUARTER], F32, name="top%d" % k) for k in range(4)]
         diff = sb.tile([P, I], F32, name="diff")
@@ -117,20 +119,17 @@ def tile_attend_exchanged_lean_twiceput_heads_kernel(
         nc.vector.tensor_copy(out=ga[0][:, 1, :], in_=a[:].indirect(entries(list2, 0, HALF)))
         nc.vector.tensor_copy(out=gb[0][:, 0, :], in_=b[:].indirect(entries(list2, 0, HALF)))
         nc.scalar.activation(gb[0][:, 1, :], b[:].indirect(entries(list1, 0, HALF)), COPY)
-        nc.scalar.activation(ga[1][:, 0, :], a[:].indirect(entries(list1, HALF, I)), COPY)
-        nc.scalar.activation(ga[1][:, 1, :], a[:].indirect(entries(list2, HALF, I)), COPY)
         nc.scalar.activation(gb[1][:, 0, :], b[:].indirect(entries(list2, HALF, I)), COPY)
         nc.scalar.activation(gb[1][:, 1, :], b[:].indirect(entries(list1, HALF, I)), COPY)
 
-        chunks = T // OUT_CHUNK
-        blocks = OUT_CHUNK // P
-        turned = [ps.tile([P, OUT_CHUNK], F32, name="turned%d" % k, tag="bank%d" % k) for k in range(chunks)]
-        for k in range(chunks):
-            for j in range(blocks):
-                c = OUT_CHUNK * k + P * j
+        turned = [
+            ps.tile([P, hi - lo], F32, name="turned%d" % k, tag="bank%d" % k) for k, (lo, hi) in enumerate(OUT_SPANS)
+        ]
+        for k, (lo, hi) in enumerate(OUT_SPANS):
+            for c in range(lo, hi, P):
                 nc.tensor.matmul(
-                    turned[k][:, P * j : P * (j + 1)], old_sb[:, c : c + P], ident[:],
-                    start=(j == 0), stop=False, is_transpose=True,
+                    turned[k][:, c - lo : c - lo + P], old_sb[:, c : c + P], ident[:],
+                    start=(c == lo), stop=False, is_transpose=True,
                 )
 
         def put(window, lst, lo, hi):
@@ -146,32 +145,32 @@ def tile_attend_exchanged_lean_twiceput_heads_kernel(
                 nc.vector.tensor_tensor(
                     diff[:, k * QUARTER : (k + 1) * QUARTER], top[k][:, 0, :], top[k][:, 1, :], ALU.subtract
                 )
-            for k in (2 * h, 2 * h + 1):
-                put(f1, list1, k * QUARTER, (k + 1) * QUARTER)
             if h == 0:
+                ga.append(sb.tile([P, 2, HALF], F32, name="ga1", tag="ga"))
+                nc.scalar.activation(ga[1][:, 0, :], a[:].indirect(entries(list1, HALF, I)), COPY)
+                nc.scalar.activation(ga[1][:, 1, :], a[:].indirect(entries(list2, HALF, I)), COPY)
+                put(f1, list1, 0, QUARTER)
                 put(f2, list3, 0, QUARTER)
+                put(f1, list1, QUARTER, HALF)
+        put(f1, list1, HALF, I)
         put(f2, list3, QUARTER, I)
 
         back = []
-        for k in range(chunks):
-            for j in range(blocks):
-                c = OUT_CHUNK * k + P * j
+        for k, (lo, hi) in enumerate(OUT_SPANS):
+            for c in range(lo, hi, P):
                 nc.tensor.matmul(
-                    turned[k][:, P * j : P * (j + 1)], f1[:, c : c + P], ident[:],
-                    start=False, stop=(j == blocks - 1), is_transpose=True,
+                    turned[k][:, c - lo : c - lo + P], f1[:, c : c + P], ident[:],
+                    start=False, stop=(c + P == hi), is_transpose=True,
                 )
-        for k in range(chunks):
-            staged = sb.tile([P, OUT_CHUNK], F32, name="staged%d" % k)
+        for k, (lo, hi) in enumerate(OUT_SPANS):
+            staged = sb.tile([P, hi - lo], F32, name="staged%d" % k)
             nc.scalar.copy(out=staged[:], in_=turned[k][:])
-            bk = ps.tile([P, OUT_CHUNK], F32, name="back%d" % k)
-            for j in range(blocks):
-                nc.tensor.transpose(bk[:, P * j : P * (j + 1)], staged[:, P * j : P * (j + 1)], ident[:])
+            bk = ps.tile([P, hi - lo], F32, name="back%d" % k, tag="bank%d" % (4 + k))
+            for c in range(0, hi - lo, P):
+                nc.tensor.transpose(bk[:, c : c + P], staged[:, c : c + P], ident[:])
             back.append(bk)
 
-        for k in range(chunks):
-            c = OUT_CHUNK * k
-            res = sb.tile([P, OUT_CHUNK], F32, name="res%d" % k)
-            nc.vector.scalar_tensor_tensor(
-                res[:], f2[:, c : c + OUT_CHUNK], share_col[:], back[k][:], ALU.mult, ALU.add
-            )
-            nc.sync.dma_start(out=out[:, c : c + OUT_CHUNK], in_=res[:])
+        for k, (lo, hi) in enumerate(OUT_SPANS):
+            res = sb.tile([P, hi - lo], F32, name="res%d" % k)
+            nc.vector.scalar_tensor_tensor(res[:], f2[:, lo:hi], share_col[:], back[k][:], ALU.mult, ALU.add)
+            nc.sync.dma_start(out=out[:, lo:hi], in_=res[:])

@@ -39,12 +39,13 @@ def tile_attend_exchanged_lean_twiceput_heads_kernel(
         nc.vector.memset(key_scale[:].bitcast(I32), 0)
 
         raw = [sb.tile([P, PACK, Q], F32, name="raw%d" % n) for n in range(2)]
-        key_words = sb.tile([P, 2 * T], U8, name="key_words", align_bytes=64)
+        key_words = [sb.tile([P, 2 * BANK], U8, name="key_words%d" % h, align_bytes=64) for h in range(2)]
         lam_col = sb.tile([P, 1], F32, name="lam_col")
         nc.sync.dma_start(out=raw[0][:], in_=query.rearrange("(p j) q -> p j q", j=PACK))
-        nc.sync.dma_start(out=key_words[:].bitcast(I32), in_=keys_words[0].bitcast(I32))
+        nc.sync.dma_start(out=key_words[0][:].bitcast(I32), in_=keys_words[0][:, : 2 * BANK].bitcast(I32))
         nc.sync.dma_start(out=raw[1][:], in_=query2.rearrange("(p j) q -> p j q", j=PACK))
-        nc.sync.dma_start(out=lam_col[:], in_=lam)
+        nc.sync.dma_start(out=key_words[1][:].bitcast(I32), in_=keys_words[0][:, 2 * BANK :].bitcast(I32))
+        nc.gpsimd.dma_start(out=lam_col[:], in_=lam)
         for quad in range(4):
             nc.scalar.dma_start(
                 out=key_scale[32 * quad : 32 * quad + 4, :].bitcast(I32),
@@ -89,7 +90,7 @@ def tile_attend_exchanged_lean_twiceput_heads_kernel(
                     out=bank[:],
                     lhsT=codes[:].bitcast(FP8X4),
                     lhsT_scale=q_scale[:],
-                    rhs=key_words[:, 2 * lo : 2 * hi].bitcast(FP4X4),
+                    rhs=key_words[lo // BANK][:, 2 * (lo % BANK) : 2 * (lo % BANK + hi - lo)].bitcast(FP4X4),
                     rhs_scale=key_scale[:, lo:hi],
                     start=True,
                     stop=True,
@@ -101,8 +102,8 @@ def tile_attend_exchanged_lean_twiceput_heads_kernel(
         b = sb.tile([P, T], F32, name="b")
         lam_row = sb.tile([P, I], F32, name="lam_row")
         nc.scalar.copy(out=lam_row[:], in_=lam_col[:].to_broadcast([P, I]))
-        nc.vector.tensor_copy(out=a[:, :BANK], in_=scores[0][0][:])
-        nc.scalar.copy(out=a[:, 512:768], in_=scores[0][1][:])
+        nc.scalar.copy(out=a[:, :BANK], in_=scores[0][0][:])
+        nc.vector.tensor_copy(out=a[:, 512:768], in_=scores[0][1][:])
         nc.vector.tensor_copy(out=a[:, 768:], in_=scores[0][2][:])
         for (lo, hi), bank in zip(SPANS[1], scores[1]):
             nc.scalar.copy(out=b[:, lo:hi], in_=bank[:])
@@ -115,12 +116,12 @@ def tile_attend_exchanged_lean_twiceput_heads_kernel(
         top = [sb.tile([P, 2, QUARTER], F32, name="top%d" % k) for k in range(4)]
         diff = sb.tile([P, I], F32, name="diff")
 
-        nc.vector.tensor_copy(out=ga[0][:, 0, :], in_=a[:].indirect(entries(list1, 0, HALF)))
-        nc.vector.tensor_copy(out=ga[0][:, 1, :], in_=a[:].indirect(entries(list2, 0, HALF)))
-        nc.vector.tensor_copy(out=gb[0][:, 0, :], in_=b[:].indirect(entries(list2, 0, HALF)))
-        nc.scalar.activation(gb[0][:, 1, :], b[:].indirect(entries(list1, 0, HALF)), COPY)
-        nc.scalar.activation(gb[1][:, 0, :], b[:].indirect(entries(list2, HALF, I)), COPY)
-        nc.scalar.activation(gb[1][:, 1, :], b[:].indirect(entries(list1, HALF, I)), COPY)
+        nc.vector.tensor_copy(out=ga[0][:, 0, :], in_=a[:].indirect(entries(list1, HALF, I)))
+        nc.vector.tensor_copy(out=ga[0][:, 1, :], in_=a[:].indirect(entries(list2, HALF, I)))
+        nc.vector.tensor_copy(out=gb[0][:, 0, :], in_=b[:].indirect(entries(list2, HALF, I)))
+        nc.scalar.activation(gb[0][:, 1, :], b[:].indirect(entries(list1, HALF, I)), COPY)
+        nc.scalar.activation(gb[1][:, 0, :], b[:].indirect(entries(list2, 0, HALF)), COPY)
+        nc.scalar.activation(gb[1][:, 1, :], b[:].indirect(entries(list1, 0, HALF)), COPY)
 
         turned = [
             ps.tile([P, hi - lo], F32, name="turned%d" % k, tag="bank%d" % k) for k, (lo, hi) in enumerate(OUT_SPANS)
@@ -137,22 +138,24 @@ def tile_attend_exchanged_lean_twiceput_heads_kernel(
                 window[:].indirect(entries(lst, lo, hi)), diff[:, lo:hi], lam_row[:, lo:hi], ALU.mult
             )
 
-        for h in range(2):
-            for k in (2 * h, 2 * h + 1):
-                part = slice(k % 2 * QUARTER, (k % 2 + 1) * QUARTER)
-                nc.vector.tensor_tensor(top[k][:], ga[h][:, :, part], gb[h][:, :, part], ALU.max)
-            for k in (2 * h, 2 * h + 1):
+        def differences(h, first):
+            for k in range(2):
+                part = slice(k * QUARTER, (k + 1) * QUARTER)
+                nc.vector.tensor_tensor(top[2 * h + k][:], ga[h][:, :, part], gb[h][:, :, part], ALU.max)
+            for k in range(2):
+                lo = first + k * QUARTER
                 nc.vector.tensor_tensor(
-                    diff[:, k * QUARTER : (k + 1) * QUARTER], top[k][:, 0, :], top[k][:, 1, :], ALU.subtract
+                    diff[:, lo : lo + QUARTER], top[2 * h + k][:, 0, :], top[2 * h + k][:, 1, :], ALU.subtract
                 )
-            if h == 0:
-                ga.append(sb.tile([P, 2, HALF], F32, name="ga1", tag="ga"))
-                nc.scalar.activation(ga[1][:, 0, :], a[:].indirect(entries(list1, HALF, I)), COPY)
-                nc.scalar.activation(ga[1][:, 1, :], a[:].indirect(entries(list2, HALF, I)), COPY)
-                put(f1, list1, 0, QUARTER)
-                put(f2, list3, 0, QUARTER)
-                put(f1, list1, QUARTER, HALF)
+
+        differences(0, HALF)
+        ga.append(sb.tile([P, 2, HALF], F32, name="ga1", tag="ga"))
+        nc.scalar.activation(ga[1][:, 0, :], a[:].indirect(entries(list1, 0, HALF)), COPY)
+        nc.scalar.activation(ga[1][:, 1, :], a[:].indirect(entries(list2, 0, HALF)), COPY)
         put(f1, list1, HALF, I)
+        differences(1, 0)
+        put(f2, list3, 0, QUARTER)
+        put(f1, list1, 0, HALF)
         put(f2, list3, QUARTER, I)
 
         back = []

from contextlib import ExitStack

import concourse.mybir as mybir
from concourse.masks import make_identity

D, T, I, Q = 512, 1024, 512, 128
FLOPS = 2 * 2 * D * T * Q

F32 = mybir.dt.float32
BF16 = mybir.dt.bfloat16
I32 = mybir.dt.int32
U32 = mybir.dt.uint32
U16 = mybir.dt.uint16
U8 = mybir.dt.uint8
FP8X4 = mybir.dt.float8_e4m3fn_x4
FP4X4 = mybir.dt.float4_e2m1fn_x4
ALU = mybir.AluOpType
COPY = mybir.ActivationFunctionType.Copy

P = 128
PACK = 4
BANK = 512
HALF = I // 2
QUARTER = I // 4
GROUP = 16
SPANS = (((0, 512), (512, 768), (768, 1024)), ((0, 256), (256, 512), (512, 768), (768, 1024)))
OUT_SPANS = ((0, 256), (256, 512), (512, 768), (768, 1024))


def tile_attend_exchanged_lean_twiceput_heads_kernel(
    tc, query, query2, keys_words, keys_scales, lam, old, share2, offs, offs2, offs3, out
):
    nc = tc.nc
    with ExitStack() as ctx:
        sb = ctx.enter_context(tc.tile_pool(name="sb", bufs=1))
        ps = ctx.enter_context(tc.psum_pool(name="ps", bufs=1))

        key_scale = sb.tile([P, T], U8, name="key_scale", align_bytes=64)
        nc.vector.memset(key_scale[:].bitcast(I32), 0)

        raw = [sb.tile([P, PACK, Q], F32, name="raw%d" % n) for n in range(2)]
        key_words = [sb.tile([P, 2 * BANK], U8, name="key_words%d" % h, align_bytes=64) for h in range(2)]
        lam_col = sb.tile([P, 1], F32, name="lam_col")
        nc.sync.dma_start(out=raw[0][:], in_=query.rearrange("(p j) q -> p j q", j=PACK))
        nc.sync.dma_start(out=key_words[0][:].bitcast(I32), in_=keys_words[0][:, : 2 * BANK].bitcast(I32))
        nc.sync.dma_start(out=raw[1][:], in_=query2.rearrange("(p j) q -> p j q", j=PACK))
        nc.sync.dma_start(out=key_words[1][:].bitcast(I32), in_=keys_words[0][:, 2 * BANK :].bitcast(I32))
        nc.gpsimd.dma_start(out=lam_col[:], in_=lam)
        for quad in range(4):
            nc.scalar.dma_start(
                out=key_scale[32 * quad : 32 * quad + 4, :].bitcast(I32),
                in_=keys_scales[0][4 * quad : 4 * quad + 4, :].bitcast(I32),
            )
        list1 = sb.tile([P, I // GROUP], U16, name="list1")
        nc.sync.dma_start(list1[:], offs)
        list2 = sb.tile([P, I // GROUP], U16, name="list2")
        nc.sync.dma_start(list2[:], offs2)
        old_sb = sb.tile([P, T], F32, name="old_sb")
        nc.sync.dma_start(out=old_sb[:], in_=old)
        list3 = sb.tile([P, I // GROUP], U16, name="list3")
        nc.sync.dma_start(list3[:], offs3)
        share_col = sb.tile([P, 1], F32, name="share_col")
        nc.sync.dma_start(out=share_col[:], in_=share2)

        f1 = sb.tile([P, T], F32, name="f1")
        f2 = sb.tile([P, T], F32, name="f2")
        nc.vector.memset(f1[:], 0.0)
        nc.vector.memset(f2[:], 0.0)
        ident = sb.tile([P, P], F32, name="ident")
        make_identity(nc, ident[:])

        scores = []
        for n in range(2):
            grouped = sb.tile([P, Q, PACK], BF16, name="grouped%d" % n, align_bytes=64)
            nc.vector.tensor_copy(
                out=grouped[:].rearrange("p (c i) j -> p c j i", i=4),
                in_=raw[n][:].rearrange("p j (c i) -> p c j i", i=4),
            )
            codes = sb.tile([P, Q], U32, name="codes%d" % n, align_bytes=64)
            q_scale = sb.tile([P, Q], U8, name="q_scale%d" % n, align_bytes=64)
            nc.vector.quantize_mx(
                out=codes[:].bitcast(FP8X4),
                scales=q_scale[:],
                in_=grouped[:].rearrange("p q j -> p (q j)"),
            )
            banks = []
            for lo, hi in SPANS[n]:
                bank = ps.tile([P, hi - lo], F32, name="score_bank%d_%d" % (n, lo), tag="bank%d" % (3 * n + len(banks)))
                nc.tensor.matmul_mx(
                    out=bank[:],
                    lhsT=codes[:].bitcast(FP8X4),
                    lhsT_scale=q_scale[:],
                    rhs=key_words[lo // BANK][:, 2 * (lo % BANK) : 2 * (lo % BANK + hi - lo)].bitcast(FP4X4),
                    rhs_scale=key_scale[:, lo:hi],
                    start=True,
                    stop=True,
                )
                banks.append(bank)
            scores.append(banks)

        a = sb.tile([P, T], F32, name="a")
        b = sb.tile([P, T], F32, name="b")
        lam_row = sb.tile([P, I], F32, name="lam_row")
        nc.scalar.copy(out=lam_row[:], in_=lam_col[:].to_broadcast([P, I]))
        nc.scalar.copy(out=a[:, :BANK], in_=scores[0][0][:])
        nc.vector.tensor_copy(out=a[:, 512:768], in_=scores[0][1][:])
        nc.vector.tensor_copy(out=a[:, 768:], in_=scores[0][2][:])
        for (lo, hi), bank in zip(SPANS[1], scores[1]):
            nc.scalar.copy(out=b[:, lo:hi], in_=bank[:])

        def entries(lst, lo, hi):
            return lst[:, lo // GROUP : hi // GROUP]

        ga = [sb.tile([P, 2, HALF], F32, name="ga0", tag="ga")]
        gb = [sb.tile([P, 2, HALF], F32, name="gb%d" % h) for h in range(2)]
        top = [sb.tile([P, 2, QUARTER], F32, name="top%d" % k) for k in range(4)]
        diff = sb.tile([P, I], F32, name="diff")

        nc.vector.tensor_copy(out=ga[0][:, 0, :], in_=a[:].indirect(entries(list1, HALF, I)))
        nc.vector.tensor_copy(out=ga[0][:, 1, :], in_=a[:].indirect(entries(list2, HALF, I)))
        nc.vector.tensor_copy(out=gb[0][:, 0, :], in_=b[:].indirect(entries(list2, HALF, I)))
        nc.scalar.activation(gb[0][:, 1, :], b[:].indirect(entries(list1, HALF, I)), COPY)
        nc.scalar.activation(gb[1][:, 0, :], b[:].indirect(entries(list2, 0, HALF)), COPY)
        nc.scalar.activation(gb[1][:, 1, :], b[:].indirect(entries(list1, 0, HALF)), COPY)

        turned = [
            ps.tile([P, hi - lo], F32, name="turned%d" % k, tag="bank%d" % k) for k, (lo, hi) in enumerate(OUT_SPANS)
        ]
        for k, (lo, hi) in enumerate(OUT_SPANS):
            for c in range(lo, hi, P):
                nc.tensor.matmul(
                    turned[k][:, c - lo : c - lo + P], old_sb[:, c : c + P], ident[:],
                    start=(c == lo), stop=False, is_transpose=True,
                )

        def put(window, lst, lo, hi):
            nc.vector.tensor_tensor(
                window[:].indirect(entries(lst, lo, hi)), diff[:, lo:hi], lam_row[:, lo:hi], ALU.mult
            )

        def differences(h, first):
            for k in range(2):
                part = slice(k * QUARTER, (k + 1) * QUARTER)
                nc.vector.tensor_tensor(top[2 * h + k][:], ga[h][:, :, part], gb[h][:, :, part], ALU.max)
            for k in range(2):
                lo = first + k * QUARTER
                nc.vector.tensor_tensor(
                    diff[:, lo : lo + QUARTER], top[2 * h + k][:, 0, :], top[2 * h + k][:, 1, :], ALU.subtract
                )

        differences(0, HALF)
        ga.append(sb.tile([P, 2, HALF], F32, name="ga1", tag="ga"))
        nc.scalar.activation(ga[1][:, 0, :], a[:].indirect(entries(list1, 0, HALF)), COPY)
        nc.scalar.activation(ga[1][:, 1, :], a[:].indirect(entries(list2, 0, HALF)), COPY)
        put(f1, list1, HALF, I)
        differences(1, 0)
        put(f2, list3, 0, QUARTER)
        put(f1, list1, 0, HALF)
        put(f2, list3, QUARTER, I)

        back = []
        for k, (lo, hi) in enumerate(OUT_SPANS):
            for c in range(lo, hi, P):
                nc.tensor.matmul(
                    turned[k][:, c - lo : c - lo + P], f1[:, c : c + P], ident[:],
                    start=False, stop=(c + P == hi), is_transpose=True,
                )
        for k, (lo, hi) in enumerate(OUT_SPANS):
            staged = sb.tile([P, hi - lo], F32, name="staged%d" % k)
            nc.scalar.copy(out=staged[:], in_=turned[k][:])
            bk = ps.tile([P, hi - lo], F32, name="back%d" % k, tag="bank%d" % (4 + k))
            for c in range(0, hi - lo, P):
                nc.tensor.transpose(bk[:, c : c + P], staged[:, c : c + P], ident[:])
            back.append(bk)

        for k, (lo, hi) in enumerate(OUT_SPANS):
            res = sb.tile([P, hi - lo], F32, name="res%d" % k)
            nc.vector.scalar_tensor_tensor(res[:], f2[:, lo:hi], share_col[:], back[k][:], ALU.mult, ALU.add)
            nc.sync.dma_start(out=out[:, lo:hi], in_=res[:])
